import numpy as np, ml_dtypes
CORES = [2,6,10,14,18,22,26,30]
N = 8
import mx_ref
BF = ml_dtypes.bfloat16
def entries(a):
    return np.ascontiguousarray(a.T).reshape(-1)
def table(e):
    return np.ascontiguousarray(np.reshape(e, (-1, 16)).T).astype(np.int32)
def f(rng, *shape):
    return mx_ref.flush((rng.standard_normal(shape, dtype=np.float32) * np.exp2(rng.integers(-2, 3, shape[:-1] + (1,)))).astype(BF))
def wide(rng, *shape, cols=0):
    v = rng.standard_normal(shape, dtype=np.float32) * np.exp2(rng.integers(-12, 13, shape)).astype(np.float32)
    if cols: v *= np.repeat(np.exp2(rng.integers(-cols, cols + 1, shape[:-2] + (1, shape[-1] // 4))) * (rng.random(shape[:-2] + (1, shape[-1] // 4)) > 0.0625), 4, axis=-1).astype(np.float32)
    return mx_ref.flush(v.astype(BF))
T, ND, CD, LM, CAPP = 1024, 64, 16, 64, 160
def lens(rng, n, total):
    a = 1 + np.minimum(LM - 1, rng.multinomial(total - n, rng.dirichlet(np.ones(n))))
    for i in rng.permutation(n): a[i] += min(LM - a[i], total - a.sum())
    return a
def places(rng, l):
    o = rng.permutation(ND); g = rng.multinomial(T - l.sum(), rng.dirichlet(np.ones(ND + 1)))
    s = np.zeros(ND, int); s[o] = np.cumsum(g[:ND]) + np.cumsum(l[o]) - l[o]
    return s
def pick(rng, l):
    p = rng.permutation(ND); a, b = p[:CD].copy(), p[CD:].copy()
    while l[a].sum() > CAPP:
        i = np.argmax(l[a]); j = rng.choice(np.flatnonzero(l[b] < l[a[i]]))
        a[i], b[j] = b[j], a[i]
    return rng.permutation(a)
def lists(rng, kind="any"):
    s, n, c = [], [], np.zeros((N, N * CD), int)
    K, J = (T - ND) // (LM - 1), (CAPP - CD) // (LM - 1)
    TT = min(T, ND // CD * CAPP)
    for q in range(N):
        d = rng.permutation(ND); l = np.ones(ND, int)
        if kind == "long": l[d[:K]] = LM
        elif kind == "full": l[d] = np.concatenate([lens(rng, CD, CAPP), lens(rng, CD, CAPP), lens(rng, ND - 2 * CD, T - 2 * CAPP)])
        elif kind == "any": l[d] = lens(rng, ND, int(rng.integers(TT - TT // 4, TT + 1)))
        s.append(table(places(rng, l))); n.append(table(l))
        for r in range(N):
            if kind == "long": e = rng.permutation(np.concatenate([rng.permutation(d[:K])[:J], rng.permutation(d[K:])[:CD - J]]))
            elif kind == "full": k = CD * int(rng.integers(0, 2)); e = rng.permutation(d[k:k + CD])
            else: e = pick(rng, l)
            c[r, CD * q:CD * q + CD] = e
    return {"st": np.stack(s), "ln": np.stack(n), "cd": np.stack([table(c[r]) for r in range(N)])}
def setup_inputs(rng):
    return {"x": f(rng, N, 128, 4 * T), "qw": f(rng, N, 128, 512), **lists(rng)}
def setup_inputs_long(rng):
    return {**setup_inputs(rng), **lists(rng, "long")}
def setup_inputs_ones(rng):
    return {**setup_inputs(rng), **lists(rng, "ones")}
def setup_inputs_full(rng):
    return {**setup_inputs(rng), **lists(rng, "full")}
def setup_inputs_below(rng):
    d = setup_inputs(rng); p = rng.permutation(N)
    s, u = rng.integers(-20, 27, N), rng.integers(-20, 28, N)
    s[p[0]] = 26; u[rng.choice(p[:-1])] = 27; s[p[-1]] = 0; u[p[-1]] = 0
    d["x"] = mx_ref.flush((-np.exp2(rng.uniform(-3, 3, (N, 128, 4 * T)) + s[:, None, None])).astype(BF))
    d["qw"] = mx_ref.flush(np.exp2(rng.uniform(-2, 2, (N, 128, 512)) + u[:, None, None]).astype(BF))
    return d
def setup_inputs_spread(rng):
    d = setup_inputs(rng); d["x"] = wide(rng, N, 128, 4 * T, cols=8); return d
def check_inputs(d):
    b = []
    L = [entries(d["ln"][r]).astype(np.int64) for r in range(N)]
    for r in range(N):
        s, l = entries(d["st"][r]).astype(np.int64), L[r]
        if l.min() < 1 or l.max() > LM: b.append("ln")
        o = np.argsort(s, kind="stable")
        if s.min() < 0 or (s + l).max() > T or (s[o][:-1] + l[o][:-1] > s[o][1:]).any(): b.append("st")
        c = entries(d["cd"][r])
        if c.min() < 0 or c.max() >= ND: b.append("cd"); continue
        for q in range(N):
            e = c[CD * q:CD * q + CD]
            if len(set(e.tolist())) != CD or L[q][e].sum() > CAPP: b.append("cd")
    return sorted(set(b))
def reference(x, qw, st, ln, cd):
    X = [mx_ref.quantize(x[q]) for q in range(N)]
    y = np.zeros((N, 128, N * CD), np.float32)
    for r in range(N):
        W = mx_ref.quantize(qw[r]); c = entries(cd[r])
        for q in range(N):
            z = mx_ref.matmul(W, X[q]); s, l = entries(st[q]), entries(ln[q])
            for i in range(CD * q, CD * q + CD):
                y[r][:, i] = z[:, s[c[i]]:s[c[i]] + l[c[i]]].max(axis=1)
    return {"y": y}

@@ -1,0 +1,334 @@
+from concourse.bass import DstId, RemoteDMATransfer
+from concourse.mybir import dt, AluOpType, ActivationFunctionType
+
+N, CD, CAP, XC = 8, 16, 160, 1024
+XW = XC + CAP
+BS = CAP + 8
+STEP = 2048
+BIG = 4.0e6
+NEG = -5.0e29
+
+SCRATCH = {k: ("sbuf", [128, w], t) for t, ks in {
+    "int32": {"cd8": 8, "cdl": 8, "sl": 128, "ip": 1, "ci": 4},
+    "float32": {"row": 192, "tab": 192, "cf": 4, "t4": CAP, "i16": 64, "kk": 16, "tri": 64, "rst": 64, "stp": CAP, "tak": CAP,
+                "tl0": 64, "tl1": 64, "o0": 64, "o1": 64, "en0": 72, "en1": 72, "sg0": 64, "sg1": 64, "d0": 72, "d1": 72,
+                "bw": 8 * BS, "fl": 8 * CAP, "gl": 8 * CAP, "ee": 8, "raw": 128, "tin": 32, "tout": 32, "ef": 16,
+                "msk": 8 * CAP + 8, "neg": 128, "z": 8 * CAP, "ys": 128},
+    "uint16": {"cu0": 4, "cu1": 4, "lu0": 8, "lu1": 8, "off": 320, "eu": 16},
+    "bfloat16": {"xs": 4 * XW, "h": 32 * CAP, "qs": 512},
+    "float8_e4m3fn_x4": {"qc": 8 * CAP, "wc": 128, "rc": 8 * CAP},
+    "uint8": {"qp": 8 * CAP, "wp": 128, "rp": 8 * CAP}}.items() for k, w in ks.items()}
+SCRATCH["es"] = ("dram", [128, 1], "float32")
+SCRATCH["el"] = ("dram", [8, 128, 1], "float32")
+SCRATCH["ps"] = ("psum", [128, 8 * 512], "float32")
+SEMAPHORES = (["ldc", "ldt", "ldx", "ldq", "gi", "pb", "vt", "xgo", "vz", "ca", "cb", "cu0", "cu1", "en0", "en1", "st0", "st1",
+               "es", "est", "er", "rw", "ell", "wq", "yd", "ls", "vv"]
+              + [n + str(s) for n in ("of", "hg", "qz", "ar", "pm", "lv") for s in range(8)] + ["yg" + str(c) for c in range(4)])
+
+SHARE = [20, 40, 40, 20, 40, 20, 40, 40]
+
+
+def rank_program(g, core, T, topo):
+    me = T.rank_of(core)
+    if me is None:
+        return
+    A, F = AluOpType, ActivationFunctionType
+    v, sc, sy, pe = g.vector, g.scalar, g.sync, g.tensor
+    S = T.sem
+    cores = list(T.cores)
+
+    def dist(a, b):
+        ca, cb = topo.chip(a), topo.chip(b)
+        if ca == cb:
+            return 3
+        if topo.mates(ca, cb):
+            return 2
+        return 1 if topo.same_plane(ca, cb) else 0
+
+    def chipmates(c):
+        return [r for r in range(N) if topo.chip(cores[r]) == topo.chip(c)]
+
+    def slot(a, b):
+        return 2 * dist(cores[a], cores[b]) + chipmates(cores[b]).index(b)
+
+    rank_at = [None] * N
+    for r in range(N):
+        rank_at[slot(me, r)] = r
+    own = slot(me, me)
+    par = [s for s in (6, 7) if s != own][0]
+    far_e = topo.engines(core, cores[rank_at[0]])
+    near_e = [e for e in topo.engines(core, cores[rank_at[par]]) if e not in far_e]
+
+    def msk(es):
+        m = 0
+        for e in es:
+            m |= 1 << e
+        return int(m)
+
+    sent = [0]
+
+    def tr(s, es, sem, src, dst):
+        rid, pid, _ = topo.addr(cores[rank_at[s]])
+        sent[0] += len(es)
+        return RemoteDMATransfer(dst_ids=[DstId(rid=rid, pnc=pid)], dma_engine_mask=msk(es), remote_sem=S[sem], src=src, dst=dst)
+
+    def there(s):
+        return slot(rank_at[s], me)
+
+    for k in range(8):
+        (sy if k % 2 == 0 else sc).dma_start(T.cd8[16 * k:16 * k + 16, :], T.cd[:, :]).then_inc(S.ldc, 16)
+    sy.dma_start(T.sl[0:1, 0:64], T.st[:, :]).then_inc(S.ldt, 16)
+    sc.dma_start(T.sl[0:1, 64:128], T.ln[:, :]).then_inc(S.ldt, 16)
+    sy.dma_start(T.xs[:, 0:1024], T.x[:, 0:1024]).then_inc(S.ldx, 16)
+    sc.dma_start(T.xs[:, 1024:2048], T.x[:, 1024:2048]).then_inc(S.ldx, 16)
+    sy.wait_ge(S.xgo, 1)
+    sy.dma_start(T.xs[:, 2048:3072], T.x[:, 2048:3072]).then_inc(S.ldx, 16)
+    sc.wait_ge(S.xgo, 1)
+    sc.dma_start(T.xs[:, 3072:4096], T.x[:, 3072:4096]).then_inc(S.ldx, 16)
+    sc.dma_start(T.qs[:, :], T.qw[:, :]).then_inc(S.ldq, 16)
+
+    g.iota(T.ip[:, 0:1], [[0, 1]], 0, 1).then_inc(S.gi, 1)
+    for out, pat, base in ((T.t4[:, :], [[0, 40], [1, 4]], 0), (T.i16[:, :], [[0, 4], [1, 16]], 0),
+                           (T.kk[:, 0:8], [[CAP, 8]], 0), (T.kk[:, 8:16], [[0, 4], [CAP, 2]], -1)):
+        g.iota(out, pat, base, 0, allow_small_or_imprecise_dtypes=True).then_inc(S.gi, 1)
+    g.wait_ge(S.ldc, 128)
+
+    def cdt(s, es, sem):
+        r, d = rank_at[s], there(s)
+        return tr(s, es, sem, T.cd8[:, r:r + 1], T.cdl[:, d:d + 1])
+    g.remote_dma_fused([cdt(s, far_e[2 * s:2 * s + 2], "ca") for s in range(4)], local_sem=S.ls)
+    g.remote_dma_fused([cdt(4, far_e[0:4], "cb"), cdt(5, far_e[4:8], "cb"), cdt(par, near_e[0:4], "cb")], local_sem=S.ls)
+    g.sem_inc(S.xgo, 1)
+    g.wait_ge(S.vt, 1)
+    g.partition_broadcast(T.tab[:, 0:192], T.row[0:1, 0:192], 128).then_inc(S.pb, 1)
+
+    n = {"vv": 0}
+
+    def op(ins):
+        ins.then_inc(S.vv, 1)
+        n["vv"] += 1
+
+    def sync_v():
+        v.wait_ge(S.vv, n["vv"])
+
+    v.memset(T.xs[:, 4 * XC:4 * XW], 0.0).then_inc(S.vz, 1)
+    op(v.memset(T.bw[:, :], 0.0))
+    for b in "01":
+        op(v.memset(T["en" + b][:, 0:1], 0.0))
+        op(v.memset(T["d" + b][:, 64:65], 0.0))
+    v.memset(T.raw[:, :], 0.0).then_inc(S.rw, 1)
+    v.wait_ge(S.gi, 5)
+    op(v.tensor_scalar(T.ci[:, 0:1], T.ip[:, 0:1], 15, None, A.bitwise_and))
+    op(v.tensor_scalar(T.ci[:, 2:3], T.ip[:, 0:1], 3, None, A.bitwise_and))
+    op(v.tensor_scalar(T.rst[:, :], T.i16[:, :], 0.0, None, A.is_gt))
+    op(v.tensor_scalar(T.stp[:, :], T.t4[:, :], 0.0, 4.0 * STEP, A.is_gt, A.mult))
+    sync_v()
+    op(v.tensor_scalar(T.ci[:, 1:2], T.ci[:, 0:1], 2, None, A.arith_shift_right))
+    op(v.tensor_scalar(T.stp[:, :], T.stp[:, :], 1.0 - 3.0 * STEP, None, A.add))
+    sync_v()
+    op(v.tensor_copy(T.cf[:, 0:3], T.ci[:, 0:3]))
+    op(v.memset(T.stp[:, 0:1], 0.0))
+    sync_v()
+    op(v.tensor_scalar(T.tri[:, :], T.i16[:, :], T.cf[:, 0:1], None, A.is_le))
+    op(v.tensor_scalar(T.tak[:, :], T.t4[:, :], T.cf[:, 1:2], BIG, A.is_equal, A.mult))
+    op(v.tensor_scalar(T.cf[:, 3:4], T.cf[:, 1:2], -4.0 * STEP, T.cf[:, 2:3], A.mult, A.add))
+    v.wait_ge(S.ldt, 32)
+    for k in range(4):
+        op(v.tensor_copy(T.row[0:1, 16 * k:16 * k + 16], T.sl[0:1, k:64:4]))
+        op(v.tensor_copy(T.row[0:1, 64 + 16 * k:80 + 16 * k], T.sl[0:1, 64 + k:128:4]))
+    sync_v()
+    v.tensor_tensor(T.row[0:1, 128:192], T.row[0:1, 0:64], T.row[0:1, 64:128], A.add).then_inc(S.vt, 1)
+    v.wait_ge(S.ldc, 128)
+    v.tensor_copy(T.cu1[:, own - 4:own - 3], T.cd8[:, me:me + 1]).then_inc(S.cu1, 1)
+    v.wait_ge(S.pb, 1)
+
+    def lists_v(b):
+        cu, lu, tl, o, en, d = [T[x + str(b)] for x in ("cu", "lu", "tl", "o", "en", "d")]
+        if b == 0:
+            v.wait_ge(S.ca, 8)
+            v.tensor_copy(cu[:, 0:4], T.cdl[:, 0:4]).then_inc(S.cu0, 1)
+            v.wait_ge(S.cu0, 1)
+        else:
+            v.wait_ge(S.cb, 12)
+            v.tensor_copy(cu[:, 0:2], T.cdl[:, 4:6]).then_inc(S.cu1, 1)
+            v.tensor_copy(cu[:, par - 4:par - 3], T.cdl[:, par:par + 1]).then_inc(S.cu1, 1)
+            v.wait_ge(S.cu1, 3)
+        op(v.tensor_tensor(tl[:, 0:64], T.tab[:, 64:128].indirect(cu[:, 0:4]), T.tri[:, 0:64], A.mult))
+        sync_v()
+        op(v.tensor_tensor_scan(o[:, :], T.rst[:, :], tl[:, :], 0.0, A.mult, A.add))
+        sync_v()
+        op(v.tensor_copy(lu[:, 0:8:2], o[:, 15:64:16]))
+        v.wait_ge(S["en%d" % b], 1)
+        op(v.tensor_tensor(d[:, 0:64], T.tab[:, 0:64].indirect(cu[:, 0:4]), en[:, 0:64], A.subtract))
+
+    def ends_v():
+        for b in (0, 1):
+            for j in (0, 1):
+                r0 = rank_at[4 * b + 2 * j]
+                v.tensor_copy(T.ee[:, r0:r0 + 2], T["o%d" % b][:, 32 * j + 15:32 * j + 32:16]).then_inc(S.es, 1)
+
+    def lists_s(b):
+        cu = T["cu%d" % b]
+        sc.wait_ge(S["cu%d" % b], 1 if b == 0 else 3)
+        sc.activation(T["en%d" % b][:, 1:65], T.tab[:, 128:192].indirect(cu[:, 0:4]), F.Copy).then_inc(S["en%d" % b], 1)
+        sc.activation(T["sg%d" % b][:, 0:64], T.tab[:, 0:64].indirect(cu[:, 0:4]), F.Copy).then_inc(S["st%d" % b], 1)
+
+    def chain(s):
+        b, j = s // 4, s % 4
+        sync_v()
+        lv = S["lv%d" % s]
+        c0, c1 = CAP * s, CAP * s + CAP
+        v.tensor_copy(T.bw[:, BS * s:BS * s + BS].indirect(T["lu%d" % b][:, 2 * j:2 * j + 1]),
+                      T["d%d" % b][:, 16 * j + 1:16 * j + 17]).then_inc(lv, 1)
+        v.wait_ge(S["st%d" % b], 1)
+        v.wait_ge(lv, 1)
+        v.tensor_tensor_scan(T.fl[:, c0:c1], T.stp[:, :], T.bw[:, BS * s:BS * s + CAP], T["sg%d" % b][:, 16 * j:16 * j + 1],
+                             A.add, A.add).then_inc(lv, 1)
+        v.wait_ge(lv, 2)
+        v.tensor_tensor_scan(T.gl[:, c0:c1], T.tak[:, :], T.fl[:, c0:c1], 0.0, A.max, A.min).then_inc(lv, 1)
+        v.wait_ge(lv, 3)
+        v.tensor_scalar(T.off[:, 40 * s:40 * s + 40], T.gl[:, c0 + 3:c1:4], 4.0, T.cf[:, 3:4], A.mult, A.add).then_inc(S["of%d" % s], 1)
+
+    first = {"v": True, "s": True}
+
+    def ready(q, key):
+        if first[key]:
+            q.wait_ge(S.ldx, 64)
+            q.wait_ge(S.vz, 1)
+            first[key] = False
+
+    def gather_s(s):
+        k = SHARE[s]
+        if k > 0:
+            ready(sc, "s")
+            sc.wait_ge(S["of%d" % s], 1)
+            sc.activation(T.h[:, 640 * s:640 * s + 16 * k], T.xs[:, 0:4 * XW].indirect(T.off[:, 40 * s:40 * s + k]), F.Copy).then_inc(S["hg%d" % s], 1)
+
+    def gather_v(s):
+        k = SHARE[s]
+        if k < 40:
+            ready(v, "v")
+            v.wait_ge(S["of%d" % s], 1)
+            v.tensor_copy(T.h[:, 640 * s + 16 * k:640 * s + 640], T.xs[:, 0:4 * XW].indirect(T.off[:, 40 * s + k:40 * s + 40])).then_inc(S["hg%d" % s], 1)
+
+    def quant(s):
+        v.wait_ge(S["hg%d" % s], int(SHARE[s] > 0) + int(SHARE[s] < 40))
+        v.quantize_mx(T.qc[:, CAP * s:CAP * s + CAP], T.qp[:, CAP * s:CAP * s + CAP], T.h[:, 640 * s:640 * s + 640]).then_inc(S["qz%d" % s], 1)
+
+    lists_s(0)
+    gather_s(0)
+    gather_s(1)
+    lists_s(1)
+    for s in (2, 3, 4, 5, par, own):
+        gather_s(s)
+
+    lists_v(0)
+    chain(0)
+    gather_v(0)
+    chain(1)
+    quant(0)
+    lists_v(1)
+    ends_v()
+    chain(2)
+    quant(1)
+    gather_v(2)
+    chain(3)
+    gather_v(3)
+    quant(2)
+    chain(4)
+    quant(3)
+    gather_v(4)
+    chain(5)
+    gather_v(5)
+    quant(4)
+    chain(par)
+    quant(5)
+    v.wait_ge(S.ldq, 16)
+    v.quantize_mx(T.wc[:, :], T.wp[:, :], T.qs[:, :]).then_inc(S.wq, 1)
+    gather_v(par)
+    chain(own)
+    quant(par)
+    gather_v(own)
+    op(v.memset(T.msk[:, :], 0.0))
+    op(v.memset(T.neg[:, :], NEG))
+    quant(own)
+
+    sy.wait_ge(S.es, 4)
+    sy.dma_start(T.es[:, :], T.ee[0:16, 0:8]).then_inc(S.est, 16)
+    sy.dma_start(T.el[me], T.ee[0:16, 0:8]).then_inc(S.est, 16)
+
+    def codes(s, es):
+        r, d = rank_at[s], there(s)
+        rid, pid, _ = topo.addr(cores[r])
+        g.wait_ge(S["qz%d" % s], 1)
+        g.remote_dma(out_ap=T.rc[:, CAP * d:CAP * d + CAP].bitcast(dt.uint8), in_ap=T.qc[:, CAP * s:CAP * s + CAP].bitcast(dt.uint8),
+                     remote_sem=S["ar%d" % d], local_sem=S.ls, pid=pid, routing_id=rid, dma_engine_mask=msk(es))
+        sent[0] += len(es)
+
+    def plane(s, es):
+        d = there(s)
+        return tr(s, es, "ar%d" % d, T.qp[:, CAP * s:CAP * s + CAP], T.rp[:, CAP * d:CAP * d + CAP])
+
+    def send_ends():
+        g.wait_ge(S.est, 32)
+        ids = []
+        for s in [0, 1, 2, 3, 4, 5, par]:
+            rid, pid, _ = topo.addr(cores[rank_at[s]])
+            ids.append(DstId(rid=rid, pnc=pid))
+        g.remote_dma_fused([RemoteDMATransfer(dst_ids=ids, dma_engine_mask=msk(far_e[0:1]), remote_sem=S.er, srcs=[T.es[:, :]],
+                                              dsts=[T.el[me] for _ in ids])], local_sem=S.ls)
+        sent[0] += 1
+
+    for s in (0, 2, 4):
+        codes(s, far_e)
+        codes(s + 1, far_e)
+        g.remote_dma_fused([plane(s, far_e[0:4]), plane(s + 1, far_e[4:8])], local_sem=S.ls)
+        if s == 2:
+            send_ends()
+    codes(par, near_e)
+    g.remote_dma_fused([plane(par, near_e)], local_sem=S.ls)
+
+    sy.wait_ge(S.est, 32)
+    sy.wait_ge(S.er, 7)
+    sy.wait_ge(S.rw, 1)
+    for a in range(4):
+        sy.dma_start(T.raw[32 * a:32 * a + 8, :], T.el[:, :, :]).then_inc(S.ell, 16)
+    v.wait_ge(S.ell, 64)
+    op(v.tensor_copy(T.tin[:, 0:16], T.raw[:, me:128:8]))
+    op(v.tensor_copy(T.tin[:, 16:32], T.raw[:, me:128:8]))
+    sync_v()
+    op(v.transpose(T.tout[:, :], T.tin[:, :]))
+    sync_v()
+    op(v.tensor_tensor(T.ef[:, 0:8], T.tout[:, 0:8], T.kk[:, 0:8], A.add))
+    op(v.tensor_tensor(T.ef[:, 8:16], T.tout[:, 0:8], T.kk[:, 8:16], A.add))
+    sync_v()
+    op(v.tensor_copy(T.eu[:, :], T.ef[:, :]))
+    sync_v()
+    op(v.tensor_copy(T.msk[:, :].indirect(T.eu[:, 0:8]), T.neg[:, :]))
+    sync_v()
+
+    pe.wait_ge(S.wq, 1)
+    order = [0, 1, 2, 3, own, par, 4, 5]
+    for s in order:
+        if s == own:
+            pe.wait_ge(S["qz%d" % own], 1)
+            c, p = T.qc, T.qp
+        else:
+            pe.wait_ge(S["ar%d" % s], 16 if s == par else 12)
+            c, p = T.rc, T.rp
+        pe.matmul_mx(T.ps[:, 512 * s:512 * s + CAP], T.wc[:, :], T.wp[:, :], c[:, CAP * s:CAP * s + CAP], p[:, CAP * s:CAP * s + CAP],
+                     True, True).then_inc(S["pm%d" % s], 1)
+    for k in range(4):
+        for s in order[2 * k:2 * k + 2]:
+            r = rank_at[s]
+            v.wait_ge(S["pm%d" % s], 1)
+            op(v.tensor_tensor_scan(T.z[:, CAP * s:CAP * s + CAP], T.msk[:, CAP * r:CAP * r + CAP], T.ps[:, 512 * s:512 * s + CAP],
+                                    NEG, A.add, A.max))
+        c = order[2 * k] // 2
+        r0 = rank_at[2 * c]
+        sync_v()
+        v.tensor_copy(T.ys[:, 16 * r0:16 * r0 + 32], T.z[:, 320 * c:320 * c + 320].indirect(T.eu[:, 8 + r0:10 + r0])).then_inc(S["yg%d" % c], 1)
+        sy.wait_ge(S["yg%d" % c], 1)
+        sy.dma_start(T.y[:, 16 * r0:16 * r0 + 32], T.ys[:, 16 * r0:16 * r0 + 32]).then_inc(S.yd, 16)
+    sy.wait_ge(S.yd, 64)
+    g.wait_ge(S.ls, sent[0])

@@ -3,29 +3,29 @@ from concourse.mybir import dt, AluOpType, ActivationFunctionType
 
 N, CD, CAP, XC = 8, 16, 160, 1024
 XW = XC + CAP
-BS = CAP + 8
-STEP = 2048
-BIG = 4.0e6
 NEG = -5.0e29
+W = N * CD
 
 SCRATCH = {k: ("sbuf", [128, w], t) for t, ks in {
-    "int32": {"cd8": 8, "cdl": 8, "sl": 128, "ip": 1, "ci": 4},
-    "float32": {"row": 192, "tab": 192, "cf": 4, "t4": CAP, "i16": 64, "kk": 16, "tri": 64, "rst": 64, "stp": CAP, "tak": CAP,
-                "tl0": 64, "tl1": 64, "o0": 64, "o1": 64, "en0": 72, "en1": 72, "sg0": 64, "sg1": 64, "d0": 72, "d1": 72,
-                "bw": 8 * BS, "fl": 8 * CAP, "gl": 8 * CAP, "ee": 8, "raw": 128, "tin": 32, "tout": 32, "ef": 16,
+    "int32": {"cd8": 8, "cdl": 32, "sl": 128, "ip": 1, "ci": 1, "ei": W, "ph": W},
+    "float32": {"row": 192, "tab": 192, "cf": 8, "kk": 24, "rst": W, "sb": W, "zz": W, "cc": W,
+                "lnf": W, "eb": W + 4, "cmpb": W + 4, "bs": W + 4, "ix": W, "jp": W, "mk": W, "gm": W, "gg": W, "hh": W,
+                "t1": W + 4, "t2": W, "raw": 16, "tin": 32, "tout": 32, "ef": 16,
                 "msk": 8 * CAP + 8, "neg": 128, "z": 8 * CAP, "ys": 128},
-    "uint16": {"cu0": 4, "cu1": 4, "lu0": 8, "lu1": 8, "off": 320, "eu": 16},
+    "uint16": {"cu": 8, "iu": 8, "of0": W, "of1": W, "of2": W, "of3": W, "eu": 16},
     "bfloat16": {"xs": 4 * XW, "h": 32 * CAP, "qs": 512},
     "float8_e4m3fn_x4": {"qc": 8 * CAP, "wc": 128, "rc": 8 * CAP},
     "uint8": {"qp": 8 * CAP, "wp": 128, "rp": 8 * CAP}}.items() for k, w in ks.items()}
 SCRATCH["es"] = ("dram", [128, 1], "float32")
 SCRATCH["el"] = ("dram", [8, 128, 1], "float32")
-SCRATCH["ps"] = ("psum", [128, 8 * 512], "float32")
-SEMAPHORES = (["ldc", "ldt", "ldx", "ldq", "gi", "pb", "vt", "xgo", "vz", "ca", "cb", "cu0", "cu1", "en0", "en1", "st0", "st1",
-               "es", "est", "er", "rw", "ell", "wq", "yd", "ls", "vv"]
-              + [n + str(s) for n in ("of", "hg", "qz", "ar", "pm", "lv") for s in range(8)] + ["yg" + str(c) for c in range(4)])
+SCRATCH["ps"] = ("psum", [128, 4 * 512], "float32")
+SEMAPHORES = (["ldc", "ldt", "ldx", "ldq", "gi", "pb", "vt", "xgo", "vz", "ca", "cb", "est", "er", "ell", "wq", "yd", "ls", "vv", "rw",
+               "e0", "e1", "e2"]
+              + [n + str(s) for n in ("hg", "qz", "ar") for s in range(8)]
+              + [n + str(s) for n in ("pm", "yg") for s in range(4)]
+              + ["of%d%d" % (b, t) for b in (0, 1) for t in range(4)] + ["m%d_%d" % (b, k) for b in (0, 1) for k in range(3, 16)])
 
-SHARE = [20, 40, 40, 20, 40, 20, 40, 40]
+SCALAR = [(0, 1), (0, 1, 2, 3), (0, 1, 2), (0, 1), (0, 1, 2), (0, 1), (0, 1, 2, 3), (0, 1)]
 
 
 def rank_program(g, core, T, topo):
@@ -88,14 +88,14 @@ def rank_program(g, core, T, topo):
     sc.dma_start(T.qs[:, :], T.qw[:, :]).then_inc(S.ldq, 16)
 
     g.iota(T.ip[:, 0:1], [[0, 1]], 0, 1).then_inc(S.gi, 1)
-    for out, pat, base in ((T.t4[:, :], [[0, 40], [1, 4]], 0), (T.i16[:, :], [[0, 4], [1, 16]], 0),
-                           (T.kk[:, 0:8], [[CAP, 8]], 0), (T.kk[:, 8:16], [[0, 4], [CAP, 2]], -1)):
+    for out, pat, base in ((T.kk[:, 0:8], [[CAP, 8]], 0), (T.kk[:, 8:16], [[0, 4], [CAP, 2]], -1), (T.kk[:, 16:24], [[0, 2], [CD, 4]], 0),
+                           (T.cc[:, :], [[0, 8], [16, 16]], -16)):
         g.iota(out, pat, base, 0, allow_small_or_imprecise_dtypes=True).then_inc(S.gi, 1)
     g.wait_ge(S.ldc, 128)
 
     def cdt(s, es, sem):
         r, d = rank_at[s], there(s)
-        return tr(s, es, sem, T.cd8[:, r:r + 1], T.cdl[:, d:d + 1])
+        return tr(s, es, sem, T.cd8[:, r:r + 1], T.cdl[:, 4 * d:4 * d + 1])
     g.remote_dma_fused([cdt(s, far_e[2 * s:2 * s + 2], "ca") for s in range(4)], local_sem=S.ls)
     g.remote_dma_fused([cdt(4, far_e[0:4], "cb"), cdt(5, far_e[4:8], "cb"), cdt(par, near_e[0:4], "cb")], local_sem=S.ls)
     g.sem_inc(S.xgo, 1)
@@ -112,26 +112,22 @@ def rank_program(g, core, T, topo):
         v.wait_ge(S.vv, n["vv"])
 
     v.memset(T.xs[:, 4 * XC:4 * XW], 0.0).then_inc(S.vz, 1)
-    op(v.memset(T.bw[:, :], 0.0))
-    for b in "01":
-        op(v.memset(T["en" + b][:, 0:1], 0.0))
-        op(v.memset(T["d" + b][:, 64:65], 0.0))
     v.memset(T.raw[:, :], 0.0).then_inc(S.rw, 1)
+    op(v.memset(T.zz[:, :], 0.0))
+    op(v.memset(T.sb[:, :], 0.0))
+    op(v.memset(T.rst[:, :], 1.0))
+    for b in ("eb", "cmpb", "bs", "t1"):
+        op(v.memset(T[b][:, 0:1], 0.0))
     v.wait_ge(S.gi, 5)
     op(v.tensor_scalar(T.ci[:, 0:1], T.ip[:, 0:1], 15, None, A.bitwise_and))
-    op(v.tensor_scalar(T.ci[:, 2:3], T.ip[:, 0:1], 3, None, A.bitwise_and))
-    op(v.tensor_scalar(T.rst[:, :], T.i16[:, :], 0.0, None, A.is_gt))
-    op(v.tensor_scalar(T.stp[:, :], T.t4[:, :], 0.0, 4.0 * STEP, A.is_gt, A.mult))
     sync_v()
-    op(v.tensor_scalar(T.ci[:, 1:2], T.ci[:, 0:1], 2, None, A.arith_shift_right))
-    op(v.tensor_scalar(T.stp[:, :], T.stp[:, :], 1.0 - 3.0 * STEP, None, A.add))
+    op(v.tensor_copy(T.cf[:, 0:1], T.ci[:, 0:1]))
+    op(v.tensor_copy(T.rst[:, 0:W:CD], T.zz[:, 0:8]))
+    op(v.tensor_copy(T.sb[:, 0:W:CD], T.kk[:, 16:24]))
     sync_v()
-    op(v.tensor_copy(T.cf[:, 0:3], T.ci[:, 0:3]))
-    op(v.memset(T.stp[:, 0:1], 0.0))
-    sync_v()
-    op(v.tensor_scalar(T.tri[:, :], T.i16[:, :], T.cf[:, 0:1], None, A.is_le))
-    op(v.tensor_scalar(T.tak[:, :], T.t4[:, :], T.cf[:, 1:2], BIG, A.is_equal, A.mult))
-    op(v.tensor_scalar(T.cf[:, 3:4], T.cf[:, 1:2], -4.0 * STEP, T.cf[:, 2:3], A.mult, A.add))
+    op(v.tensor_scalar(T.cf[:, 1:2], T.cf[:, 0:1], 16.0, -16.0, A.mult, A.add))
+    for t in range(4):
+        op(v.tensor_scalar(T.cf[:, 2 + t:3 + t], T.cf[:, 0:1], 4.0, float(t), A.mult, A.add))
     v.wait_ge(S.ldt, 32)
     for k in range(4):
         op(v.tensor_copy(T.row[0:1, 16 * k:16 * k + 16], T.sl[0:1, k:64:4]))
@@ -139,163 +135,150 @@ def rank_program(g, core, T, topo):
     sync_v()
     v.tensor_tensor(T.row[0:1, 128:192], T.row[0:1, 0:64], T.row[0:1, 64:128], A.add).then_inc(S.vt, 1)
     v.wait_ge(S.ldc, 128)
-    v.tensor_copy(T.cu1[:, own - 4:own - 3], T.cd8[:, me:me + 1]).then_inc(S.cu1, 1)
+    op(v.tensor_copy(T.cdl[:, 4 * own:4 * own + 1], T.cd8[:, me:me + 1]))
+    op(v.memset(T.neg[:, :], NEG))
+    op(v.memset(T.msk[:, :], 0.0))
+    sync_v()
+    op(v.tensor_copy(T.msk[:, 0:8 * CAP:CAP], T.neg[:, 0:8]))
+    sync_v()
+
+    v.wait_ge(S.ca, 8)
+    v.wait_ge(S.cb, 12)
+    v.tensor_copy(T.cu[:, 0:8], T.cdl[:, 0:32:4]).then_inc(S.e0, 1)
     v.wait_ge(S.pb, 1)
+    v.wait_ge(S.e0, 1)
+    v.tensor_copy(T.lnf[:, :], T.tab[:, 64:128].indirect(T.cu[:, 0:8])).then_inc(S.e1, 1)
+    v.wait_ge(S.e1, 1)
+    v.tensor_tensor_scan(T.eb[:, 1:W + 1], T.rst[:, :], T.lnf[:, :], 0.0, A.mult, A.add).then_inc(S.e2, 1)
+    v.wait_ge(S.e2, 1)
 
-    def lists_v(b):
-        cu, lu, tl, o, en, d = [T[x + str(b)] for x in ("cu", "lu", "tl", "o", "en", "d")]
-        if b == 0:
-            v.wait_ge(S.ca, 8)
-            v.tensor_copy(cu[:, 0:4], T.cdl[:, 0:4]).then_inc(S.cu0, 1)
-            v.wait_ge(S.cu0, 1)
-        else:
-            v.wait_ge(S.cb, 12)
-            v.tensor_copy(cu[:, 0:2], T.cdl[:, 4:6]).then_inc(S.cu1, 1)
-            v.tensor_copy(cu[:, par - 4:par - 3], T.cdl[:, par:par + 1]).then_inc(S.cu1, 1)
-            v.wait_ge(S.cu1, 3)
-        op(v.tensor_tensor(tl[:, 0:64], T.tab[:, 64:128].indirect(cu[:, 0:4]), T.tri[:, 0:64], A.mult))
-        sync_v()
-        op(v.tensor_tensor_scan(o[:, :], T.rst[:, :], tl[:, :], 0.0, A.mult, A.add))
-        sync_v()
-        op(v.tensor_copy(lu[:, 0:8:2], o[:, 15:64:16]))
-        v.wait_ge(S["en%d" % b], 1)
-        op(v.tensor_tensor(d[:, 0:64], T.tab[:, 0:64].indirect(cu[:, 0:4]), en[:, 0:64], A.subtract))
+    def lists(b, between=None):
+        lo, hi, c0, c1 = 64 * b, 64 * b + 64, 4 * b, 4 * b + 4
 
-    def ends_v():
-        for b in (0, 1):
-            for j in (0, 1):
-                r0 = rank_at[4 * b + 2 * j]
-                v.tensor_copy(T.ee[:, r0:r0 + 2], T["o%d" % b][:, 32 * j + 15:32 * j + 32:16]).then_inc(S.es, 1)
+        def m(k, ins):
+            ins.then_inc(S["m%d_%d" % (b, k)], 1)
 
-    def lists_s(b):
-        cu = T["cu%d" % b]
-        sc.wait_ge(S["cu%d" % b], 1 if b == 0 else 3)
-        sc.activation(T["en%d" % b][:, 1:65], T.tab[:, 128:192].indirect(cu[:, 0:4]), F.Copy).then_inc(S["en%d" % b], 1)
-        sc.activation(T["sg%d" % b][:, 0:64], T.tab[:, 0:64].indirect(cu[:, 0:4]), F.Copy).then_inc(S["st%d" % b], 1)
+        def wm(*ks):
+            for k in ks:
+                v.wait_ge(S["m%d_%d" % (b, k)], 1)
 
-    def chain(s):
-        b, j = s // 4, s % 4
-        sync_v()
-        lv = S["lv%d" % s]
-        c0, c1 = CAP * s, CAP * s + CAP
-        v.tensor_copy(T.bw[:, BS * s:BS * s + BS].indirect(T["lu%d" % b][:, 2 * j:2 * j + 1]),
-                      T["d%d" % b][:, 16 * j + 1:16 * j + 17]).then_inc(lv, 1)
-        v.wait_ge(S["st%d" % b], 1)
-        v.wait_ge(lv, 1)
-        v.tensor_tensor_scan(T.fl[:, c0:c1], T.stp[:, :], T.bw[:, BS * s:BS * s + CAP], T["sg%d" % b][:, 16 * j:16 * j + 1],
-                             A.add, A.add).then_inc(lv, 1)
-        v.wait_ge(lv, 2)
-        v.tensor_tensor_scan(T.gl[:, c0:c1], T.tak[:, :], T.fl[:, c0:c1], 0.0, A.max, A.min).then_inc(lv, 1)
-        v.wait_ge(lv, 3)
-        v.tensor_scalar(T.off[:, 40 * s:40 * s + 40], T.gl[:, c0 + 3:c1:4], 4.0, T.cf[:, 3:4], A.mult, A.add).then_inc(S["of%d" % s], 1)
+        m(3, v.tensor_copy(T.ei[:, lo:hi], T.eb[:, lo:hi]))
+        m(4, v.tensor_scalar(T.cmpb[:, lo + 1:hi + 1], T.eb[:, lo + 1:hi + 1], T.cf[:, 1:2], None, A.is_lt))
+        m(5, v.tensor_tensor(T.bs[:, lo + 1:hi + 1], T.tab[:, 128:192].indirect(T.cu[:, c0:c1]), T.eb[:, lo + 1:hi + 1], A.subtract))
+        wm(3)
+        m(6, v.tensor_scalar(T.ph[:, lo:hi], T.ei[:, lo:hi], 15, None, A.bitwise_and))
+        wm(4)
+        m(7, v.tensor_tensor_scan(T.ix[:, lo:hi], T.cmpb[:, lo:hi], T.sb[:, lo:hi], -1.0, A.add, A.max))
+        wm(5)
+        m(8, v.tensor_tensor(T.jp[:, lo:hi], T.bs[:, lo + 1:hi + 1], T.bs[:, lo:hi], A.subtract))
+        wm(6)
+        m(9, v.tensor_scalar(T.mk[:, lo:hi], T.ph[:, lo:hi], T.cf[:, 0:1], None, A.is_le))
+        wm(7)
+        m(10, v.tensor_copy(T.iu[:, c0:c1], T.ix[:, lo + CD - 1:hi:CD]))
+        wm(8, 9)
+        m(11, v.tensor_tensor(T.gm[:, lo:hi], T.jp[:, lo:hi], T.mk[:, lo:hi], A.mult))
+        wm(11)
+        m(12, v.tensor_tensor_scan(T.gg[:, lo:hi], T.zz[:, lo:hi], T.gm[:, lo:hi], 0.0, A.add, A.add))
+        wm(12)
+        m(13, v.tensor_tensor(T.hh[:, lo:hi], T.bs[:, lo + 1:hi + 1], T.gg[:, lo:hi], A.subtract))
+        if between is not None:
+            between()
+        wm(10, 13)
+        m(14, v.tensor_tensor(T.t1[:, lo + 1:hi + 1], T.hh[:, lo:hi].indirect(T.iu[:, c0:c1]), T.cc[:, lo:hi], A.add))
+        wm(14)
+        m(15, v.tensor_tensor(T.t2[:, lo:hi], T.gg[:, lo:hi].indirect(T.iu[:, c0:c1]), T.t1[:, lo:hi], A.add))
+        wm(15)
+        for t in range(4):
+            v.tensor_scalar(T["of%d" % t][:, lo:hi], T.t2[:, lo:hi], 4.0, T.cf[:, 2 + t:3 + t], A.mult, A.add).then_inc(S["of%d%d" % (b, t)], 1)
 
-    first = {"v": True, "s": True}
+    seen = {"s": [], "v": []}
 
-    def ready(q, key):
-        if first[key]:
-            q.wait_ge(S.ldx, 64)
-            q.wait_ge(S.vz, 1)
-            first[key] = False
-
-    def gather_s(s):
-        k = SHARE[s]
-        if k > 0:
-            ready(sc, "s")
-            sc.wait_ge(S["of%d" % s], 1)
-            sc.activation(T.h[:, 640 * s:640 * s + 16 * k], T.xs[:, 0:4 * XW].indirect(T.off[:, 40 * s:40 * s + k]), F.Copy).then_inc(S["hg%d" % s], 1)
-
-    def gather_v(s):
-        k = SHARE[s]
-        if k < 40:
-            ready(v, "v")
-            v.wait_ge(S["of%d" % s], 1)
-            v.tensor_copy(T.h[:, 640 * s + 16 * k:640 * s + 640], T.xs[:, 0:4 * XW].indirect(T.off[:, 40 * s + k:40 * s + 40])).then_inc(S["hg%d" % s], 1)
+    def gather(key, s):
+        q = sc if key == "s" else v
+        role = 6 if s == own else 7 if s == par else s
+        for t in range(4):
+            if (t in SCALAR[role]) != (key == "s"):
+                continue
+            if not seen[key]:
+                q.wait_ge(S.ldx, 64)
+                q.wait_ge(S.vz, 1)
+            sem = "of%d%d" % (s // 4, t)
+            if sem not in seen[key]:
+                q.wait_ge(S[sem], 1)
+                seen[key].append(sem)
+            out, win = T.h[:, 640 * s + t:640 * s + 640:4], T.xs[:, 0:4 * XW].indirect(T["of%d" % t][:, CD * s + 2:CD * s + 12])
+            ins = sc.activation(out, win, F.Copy) if key == "s" else v.tensor_copy(out, win)
+            ins.then_inc(S["hg%d" % s], 1)
 
     def quant(s):
-        v.wait_ge(S["hg%d" % s], int(SHARE[s] > 0) + int(SHARE[s] < 40))
-        v.quantize_mx(T.qc[:, CAP * s:CAP * s + CAP], T.qp[:, CAP * s:CAP * s + CAP], T.h[:, 640 * s:640 * s + 640]).then_inc(S["qz%d" % s], 1)
+        v.wait_ge(S["hg%d" % s], 4)
+        cc, pp = (T.rc, T.rp) if s == own else (T.qc, T.qp)
+        v.quantize_mx(cc[:, CAP * s:CAP * s + CAP], pp[:, CAP * s:CAP * s + CAP], T.h[:, 640 * s:640 * s + 640]).then_inc(S["qz%d" % s], 1)
 
-    lists_s(0)
-    gather_s(0)
-    gather_s(1)
-    lists_s(1)
-    for s in (2, 3, 4, 5, par, own):
-        gather_s(s)
+    for s in (0, 1, 2, 3, 4, 5, par, own):
+        gather("s", s)
 
-    lists_v(0)
-    chain(0)
-    gather_v(0)
-    chain(1)
+    lists(0)
+    gather("v", 0)
     quant(0)
-    lists_v(1)
-    ends_v()
-    chain(2)
-    quant(1)
-    gather_v(2)
-    chain(3)
-    gather_v(3)
-    quant(2)
-    chain(4)
-    quant(3)
-    gather_v(4)
-    chain(5)
-    gather_v(5)
-    quant(4)
-    chain(par)
-    quant(5)
+    gather("v", 1)
+    lists(1, lambda: quant(1))
+    for s in (2, 4):
+        gather("v", s)
+        gather("v", s + 1)
+        quant(s)
+        quant(s + 1)
+    gather("v", par)
     v.wait_ge(S.ldq, 16)
     v.quantize_mx(T.wc[:, :], T.wp[:, :], T.qs[:, :]).then_inc(S.wq, 1)
-    gather_v(par)
-    chain(own)
     quant(par)
-    gather_v(own)
-    op(v.memset(T.msk[:, :], 0.0))
-    op(v.memset(T.neg[:, :], NEG))
-    quant(own)
+    gather("v", own)
 
-    sy.wait_ge(S.es, 4)
-    sy.dma_start(T.es[:, :], T.ee[0:16, 0:8]).then_inc(S.est, 16)
-    sy.dma_start(T.el[me], T.ee[0:16, 0:8]).then_inc(S.est, 16)
+    sy.wait_ge(S.e2, 1)
+    for d in range(4):
+        e0 = CD * rank_at[2 * d]
+        sy.dma_start(T.es[e0:e0 + 32, :], T.eb[0:1, 32 * d + 1:32 * d + 33]).then_inc(S.est, 16)
+    sy.dma_start(T.el[me, CD * me:CD * me + CD, :], T.eb[0:1, CD * own + 1:CD * own + CD + 1]).then_inc(S.est, 16)
+
+    g.wait_ge(S.est, 80)
+    ids = []
+    for s in [0, 1, 2, 3, 4, 5, par]:
+        rid, pid, _ = topo.addr(cores[rank_at[s]])
+        ids.append(DstId(rid=rid, pnc=pid))
+    g.remote_dma_fused([RemoteDMATransfer(dst_ids=ids, dma_engine_mask=msk(far_e[0:1]), remote_sem=S.er, srcs=[T.es[:, :]],
+                                          dsts=[T.el[me] for _ in ids])], local_sem=S.ls)
+    sent[0] += 1
 
     def codes(s, es):
-        r, d = rank_at[s], there(s)
-        rid, pid, _ = topo.addr(cores[r])
-        g.wait_ge(S["qz%d" % s], 1)
-        g.remote_dma(out_ap=T.rc[:, CAP * d:CAP * d + CAP].bitcast(dt.uint8), in_ap=T.qc[:, CAP * s:CAP * s + CAP].bitcast(dt.uint8),
-                     remote_sem=S["ar%d" % d], local_sem=S.ls, pid=pid, routing_id=rid, dma_engine_mask=msk(es))
-        sent[0] += len(es)
+        d = there(s)
+        return tr(s, es, "ar%d" % d, T.qc[:, CAP * s:CAP * s + CAP].bitcast(dt.uint8), T.rc[:, CAP * d:CAP * d + CAP].bitcast(dt.uint8))
 
     def plane(s, es):
         d = there(s)
         return tr(s, es, "ar%d" % d, T.qp[:, CAP * s:CAP * s + CAP], T.rp[:, CAP * d:CAP * d + CAP])
 
-    def send_ends():
-        g.wait_ge(S.est, 32)
-        ids = []
-        for s in [0, 1, 2, 3, 4, 5, par]:
-            rid, pid, _ = topo.addr(cores[rank_at[s]])
-            ids.append(DstId(rid=rid, pnc=pid))
-        g.remote_dma_fused([RemoteDMATransfer(dst_ids=ids, dma_engine_mask=msk(far_e[0:1]), remote_sem=S.er, srcs=[T.es[:, :]],
-                                              dsts=[T.el[me] for _ in ids])], local_sem=S.ls)
-        sent[0] += 1
-
     for s in (0, 2, 4):
-        codes(s, far_e)
-        codes(s + 1, far_e)
+        g.wait_ge(S["qz%d" % s], 1)
+        if s == 0:
+            g.remote_dma_fused([codes(0, far_e)], local_sem=S.ls)
+            g.wait_ge(S.qz1, 1)
+            g.remote_dma_fused([codes(1, far_e)], local_sem=S.ls)
+        else:
+            g.wait_ge(S["qz%d" % (s + 1)], 1)
+            g.remote_dma_fused([codes(s, far_e[0:4]), codes(s + 1, far_e[4:8])], local_sem=S.ls)
         g.remote_dma_fused([plane(s, far_e[0:4]), plane(s + 1, far_e[4:8])], local_sem=S.ls)
-        if s == 2:
-            send_ends()
-    codes(par, near_e)
+    g.wait_ge(S["qz%d" % par], 1)
+    g.remote_dma_fused([codes(par, near_e)], local_sem=S.ls)
     g.remote_dma_fused([plane(par, near_e)], local_sem=S.ls)
 
-    sy.wait_ge(S.est, 32)
+    sy.wait_ge(S.est, 80)
     sy.wait_ge(S.er, 7)
     sy.wait_ge(S.rw, 1)
     for a in range(4):
-        sy.dma_start(T.raw[32 * a:32 * a + 8, :], T.el[:, :, :]).then_inc(S.ell, 16)
+        sy.dma_start(T.raw[32 * a:32 * a + 8, :], T.el[:, CD * me:CD * me + CD, :]).then_inc(S.ell, 16)
     v.wait_ge(S.ell, 64)
-    op(v.tensor_copy(T.tin[:, 0:16], T.raw[:, me:128:8]))
-    op(v.tensor_copy(T.tin[:, 16:32], T.raw[:, me:128:8]))
+    op(v.tensor_copy(T.tin[:, 0:16], T.raw[:, :]))
+    op(v.tensor_copy(T.tin[:, 16:32], T.raw[:, :]))
     sync_v()
     op(v.transpose(T.tout[:, :], T.tin[:, :]))
     sync_v()
@@ -305,27 +288,24 @@ def rank_program(g, core, T, topo):
     op(v.tensor_copy(T.eu[:, :], T.ef[:, :]))
     sync_v()
     op(v.tensor_copy(T.msk[:, :].indirect(T.eu[:, 0:8]), T.neg[:, :]))
+    quant(own)
     sync_v()
 
     pe.wait_ge(S.wq, 1)
-    order = [0, 1, 2, 3, own, par, 4, 5]
-    for s in order:
-        if s == own:
-            pe.wait_ge(S["qz%d" % own], 1)
-            c, p = T.qc, T.qp
-        else:
-            pe.wait_ge(S["ar%d" % s], 16 if s == par else 12)
-            c, p = T.rc, T.rp
-        pe.matmul_mx(T.ps[:, 512 * s:512 * s + CAP], T.wc[:, :], T.wp[:, :], c[:, CAP * s:CAP * s + CAP], p[:, CAP * s:CAP * s + CAP],
-                     True, True).then_inc(S["pm%d" % s], 1)
-    for k in range(4):
-        for s in order[2 * k:2 * k + 2]:
-            r = rank_at[s]
-            v.wait_ge(S["pm%d" % s], 1)
-            op(v.tensor_tensor_scan(T.z[:, CAP * s:CAP * s + CAP], T.msk[:, CAP * r:CAP * r + CAP], T.ps[:, 512 * s:512 * s + CAP],
-                                    NEG, A.add, A.max))
-        c = order[2 * k] // 2
+    order = [0, 1, 3, 2]
+    for c in order:
+        for s in (2 * c, 2 * c + 1):
+            if s == own:
+                pe.wait_ge(S["qz%d" % own], 1)
+            else:
+                pe.wait_ge(S["ar%d" % s], 16 if s == par else 12 if c == 0 else 8)
+        pe.matmul_mx(T.ps[:, 512 * c:512 * c + 2 * CAP], T.wc[:, :], T.wp[:, :], T.rc[:, 2 * CAP * c:2 * CAP * c + 2 * CAP],
+                     T.rp[:, 2 * CAP * c:2 * CAP * c + 2 * CAP], True, True).then_inc(S["pm%d" % c], 1)
+    for c in order:
         r0 = rank_at[2 * c]
+        v.wait_ge(S["pm%d" % c], 1)
+        op(v.tensor_tensor_scan(T.z[:, 320 * c:320 * c + 320], T.msk[:, CAP * r0:CAP * r0 + 320], T.ps[:, 512 * c:512 * c + 320],
+                                NEG, A.add, A.max))
         sync_v()
         v.tensor_copy(T.ys[:, 16 * r0:16 * r0 + 32], T.z[:, 320 * c:320 * c + 320].indirect(T.eu[:, 8 + r0:10 + r0])).then_inc(S["yg%d" % c], 1)
         sy.wait_ge(S["yg%d" % c], 1)

from concourse.bass import DstId, RemoteDMATransfer
from concourse.mybir import dt, AluOpType, ActivationFunctionType

N, CD, CAP, XC = 8, 16, 160, 1024
XW = XC + CAP
NEG = -5.0e29
W = N * CD

SCRATCH = {k: ("sbuf", [128, w], t) for t, ks in {
    "int32": {"cd8": 8, "cdl": 32, "sl": 128, "ip": 1, "ci": 1, "ei": W, "ph": W},
    "float32": {"row": 192, "tab": 192, "cf": 8, "kk": 24, "rst": W, "sb": W, "zz": W, "cc": W,
                "lnf": W, "eb": W + 4, "cmpb": W + 4, "bs": W + 4, "ix": W, "jp": W, "mk": W, "gm": W, "gg": W, "hh": W,
                "t1": W + 4, "t2": W, "raw": 16, "tin": 32, "tout": 32, "ef": 16,
                "msk": 8 * CAP + 8, "neg": 128, "z": 8 * CAP, "ys": 128},
    "uint16": {"cu": 8, "iu": 8, "of0": W, "of1": W, "of2": W, "of3": W, "eu": 16},
    "bfloat16": {"xs": 4 * XW, "h": 32 * CAP, "qs": 512},
    "float8_e4m3fn_x4": {"qc": 8 * CAP, "wc": 128, "rc": 8 * CAP},
    "uint8": {"qp": 8 * CAP, "wp": 128, "rp": 8 * CAP}}.items() for k, w in ks.items()}
SCRATCH["es"] = ("dram", [128, 1], "float32")
SCRATCH["el"] = ("dram", [8, 128, 1], "float32")
SCRATCH["ps"] = ("psum", [128, 4 * 512], "float32")
SEMAPHORES = (["ldc", "ldt", "ldx", "ldq", "gi", "pb", "vt", "xgo", "vz", "ca", "cb", "est", "er", "ell", "wq", "yd", "ls", "vv", "rw",
               "e0", "e1", "e2"]
              + [n + str(s) for n in ("hg", "qz", "ar") for s in range(8)]
              + [n + str(s) for n in ("pm", "yg") for s in range(4)]
              + ["of%d%d" % (b, t) for b in (0, 1) for t in range(4)] + ["m%d_%d" % (b, k) for b in (0, 1) for k in range(3, 16)])

SCALAR = [(0, 1), (0, 1, 2, 3), (0, 1, 2), (0, 1), (0, 1, 2), (0, 1), (0, 1, 2, 3), (0, 1)]


def rank_program(g, core, T, topo):
    me = T.rank_of(core)
    if me is None:
        return
    A, F = AluOpType, ActivationFunctionType
    v, sc, sy, pe = g.vector, g.scalar, g.sync, g.tensor
    S = T.sem
    cores = list(T.cores)

    def dist(a, b):
        ca, cb = topo.chip(a), topo.chip(b)
        if ca == cb:
            return 3
        if topo.mates(ca, cb):
            return 2
        return 1 if topo.same_plane(ca, cb) else 0

    def chipmates(c):
        return [r for r in range(N) if topo.chip(cores[r]) == topo.chip(c)]

    def slot(a, b):
        return 2 * dist(cores[a], cores[b]) + chipmates(cores[b]).index(b)

    rank_at = [None] * N
    for r in range(N):
        rank_at[slot(me, r)] = r
    own = slot(me, me)
    par = [s for s in (6, 7) if s != own][0]
    far_e = topo.engines(core, cores[rank_at[0]])
    near_e = [e for e in topo.engines(core, cores[rank_at[par]]) if e not in far_e]

    def msk(es):
        m = 0
        for e in es:
            m |= 1 << e
        return int(m)

    sent = [0]

    def tr(s, es, sem, src, dst):
        rid, pid, _ = topo.addr(cores[rank_at[s]])
        sent[0] += len(es)
        return RemoteDMATransfer(dst_ids=[DstId(rid=rid, pnc=pid)], dma_engine_mask=msk(es), remote_sem=S[sem], src=src, dst=dst)

    def there(s):
        return slot(rank_at[s], me)

    for k in range(8):
        (sy if k % 2 == 0 else sc).dma_start(T.cd8[16 * k:16 * k + 16, :], T.cd[:, :]).then_inc(S.ldc, 16)
    sy.dma_start(T.sl[0:1, 0:64], T.st[:, :]).then_inc(S.ldt, 16)
    sc.dma_start(T.sl[0:1, 64:128], T.ln[:, :]).then_inc(S.ldt, 16)
    sy.dma_start(T.xs[:, 0:1024], T.x[:, 0:1024]).then_inc(S.ldx, 16)
    sc.dma_start(T.xs[:, 1024:2048], T.x[:, 1024:2048]).then_inc(S.ldx, 16)
    sy.wait_ge(S.xgo, 1)
    sy.dma_start(T.xs[:, 2048:3072], T.x[:, 2048:3072]).then_inc(S.ldx, 16)
    sc.wait_ge(S.xgo, 1)
    sc.dma_start(T.xs[:, 3072:4096], T.x[:, 3072:4096]).then_inc(S.ldx, 16)
    sc.dma_start(T.qs[:, :], T.qw[:, :]).then_inc(S.ldq, 16)

    g.iota(T.ip[:, 0:1], [[0, 1]], 0, 1).then_inc(S.gi, 1)
    for out, pat, base in ((T.kk[:, 0:8], [[CAP, 8]], 0), (T.kk[:, 8:16], [[0, 4], [CAP, 2]], -1), (T.kk[:, 16:24], [[0, 2], [CD, 4]], 0),
                           (T.cc[:, :], [[0, 8], [16, 16]], -16)):
        g.iota(out, pat, base, 0, allow_small_or_imprecise_dtypes=True).then_inc(S.gi, 1)
    g.wait_ge(S.ldc, 128)

    def cdt(s, es, sem):
        r, d = rank_at[s], there(s)
        return tr(s, es, sem, T.cd8[:, r:r + 1], T.cdl[:, 4 * d:4 * d + 1])
    g.remote_dma_fused([cdt(s, far_e[2 * s:2 * s + 2], "ca") for s in range(4)], local_sem=S.ls)
    g.remote_dma_fused([cdt(4, far_e[0:4], "cb"), cdt(5, far_e[4:8], "cb"), cdt(par, near_e[0:4], "cb")], local_sem=S.ls)
    g.sem_inc(S.xgo, 1)
    g.wait_ge(S.vt, 1)
    g.partition_broadcast(T.tab[:, 0:192], T.row[0:1, 0:192], 128).then_inc(S.pb, 1)

    n = {"vv": 0}

    def op(ins):
        ins.then_inc(S.vv, 1)
        n["vv"] += 1

    def sync_v():
        v.wait_ge(S.vv, n["vv"])

    v.memset(T.xs[:, 4 * XC:4 * XW], 0.0).then_inc(S.vz, 1)
    v.memset(T.raw[:, :], 0.0).then_inc(S.rw, 1)
    op(v.memset(T.zz[:, :], 0.0))
    op(v.memset(T.sb[:, :], 0.0))
    op(v.memset(T.rst[:, :], 1.0))
    for b in ("eb", "cmpb", "bs", "t1"):
        op(v.memset(T[b][:, 0:1], 0.0))
    v.wait_ge(S.gi, 5)
    op(v.tensor_scalar(T.ci[:, 0:1], T.ip[:, 0:1], 15, None, A.bitwise_and))
    sync_v()
    op(v.tensor_copy(T.cf[:, 0:1], T.ci[:, 0:1]))
    op(v.tensor_copy(T.rst[:, 0:W:CD], T.zz[:, 0:8]))
    op(v.tensor_copy(T.sb[:, 0:W:CD], T.kk[:, 16:24]))
    sync_v()
    op(v.tensor_scalar(T.cf[:, 1:2], T.cf[:, 0:1], 16.0, -16.0, A.mult, A.add))
    for t in range(4):
        op(v.tensor_scalar(T.cf[:, 2 + t:3 + t], T.cf[:, 0:1], 4.0, float(t), A.mult, A.add))
    v.wait_ge(S.ldt, 32)
    for k in range(4):
        op(v.tensor_copy(T.row[0:1, 16 * k:16 * k + 16], T.sl[0:1, k:64:4]))
        op(v.tensor_copy(T.row[0:1, 64 + 16 * k:80 + 16 * k], T.sl[0:1, 64 + k:128:4]))
    sync_v()
    v.tensor_tensor(T.row[0:1, 128:192], T.row[0:1, 0:64], T.row[0:1, 64:128], A.add).then_inc(S.vt, 1)
    v.wait_ge(S.ldc, 128)
    op(v.tensor_copy(T.cdl[:, 4 * own:4 * own + 1], T.cd8[:, me:me + 1]))
    op(v.memset(T.neg[:, :], NEG))
    op(v.memset(T.msk[:, :], 0.0))
    sync_v()
    op(v.tensor_copy(T.msk[:, 0:8 * CAP:CAP], T.neg[:, 0:8]))
    sync_v()

    v.wait_ge(S.ca, 8)
    v.wait_ge(S.cb, 12)
    v.tensor_copy(T.cu[:, 0:8], T.cdl[:, 0:32:4]).then_inc(S.e0, 1)
    v.wait_ge(S.pb, 1)
    v.wait_ge(S.e0, 1)
    v.tensor_copy(T.lnf[:, :], T.tab[:, 64:128].indirect(T.cu[:, 0:8])).then_inc(S.e1, 1)
    v.wait_ge(S.e1, 1)
    v.tensor_tensor_scan(T.eb[:, 1:W + 1], T.rst[:, :], T.lnf[:, :], 0.0, A.mult, A.add).then_inc(S.e2, 1)
    v.wait_ge(S.e2, 1)

    def lists(b, between=None):
        lo, hi, c0, c1 = 64 * b, 64 * b + 64, 4 * b, 4 * b + 4

        def m(k, ins):
            ins.then_inc(S["m%d_%d" % (b, k)], 1)

        def wm(*ks):
            for k in ks:
                v.wait_ge(S["m%d_%d" % (b, k)], 1)

        m(3, v.tensor_copy(T.ei[:, lo:hi], T.eb[:, lo:hi]))
        m(4, v.tensor_scalar(T.cmpb[:, lo + 1:hi + 1], T.eb[:, lo + 1:hi + 1], T.cf[:, 1:2], None, A.is_lt))
        m(5, v.tensor_tensor(T.bs[:, lo + 1:hi + 1], T.tab[:, 128:192].indirect(T.cu[:, c0:c1]), T.eb[:, lo + 1:hi + 1], A.subtract))
        wm(3)
        m(6, v.tensor_scalar(T.ph[:, lo:hi], T.ei[:, lo:hi], 15, None, A.bitwise_and))
        wm(4)
        m(7, v.tensor_tensor_scan(T.ix[:, lo:hi], T.cmpb[:, lo:hi], T.sb[:, lo:hi], -1.0, A.add, A.max))
        wm(5)
        m(8, v.tensor_tensor(T.jp[:, lo:hi], T.bs[:, lo + 1:hi + 1], T.bs[:, lo:hi], A.subtract))
        wm(6)
        m(9, v.tensor_scalar(T.mk[:, lo:hi], T.ph[:, lo:hi], T.cf[:, 0:1], None, A.is_le))
        wm(7)
        m(10, v.tensor_copy(T.iu[:, c0:c1], T.ix[:, lo + CD - 1:hi:CD]))
        wm(8, 9)
        m(11, v.tensor_tensor(T.gm[:, lo:hi], T.jp[:, lo:hi], T.mk[:, lo:hi], A.mult))
        wm(11)
        m(12, v.tensor_tensor_scan(T.gg[:, lo:hi], T.zz[:, lo:hi], T.gm[:, lo:hi], 0.0, A.add, A.add))
        wm(12)
        m(13, v.tensor_tensor(T.hh[:, lo:hi], T.bs[:, lo + 1:hi + 1], T.gg[:, lo:hi], A.subtract))
        if between is not None:
            between()
        wm(10, 13)
        m(14, v.tensor_tensor(T.t1[:, lo + 1:hi + 1], T.hh[:, lo:hi].indirect(T.iu[:, c0:c1]), T.cc[:, lo:hi], A.add))
        wm(14)
        m(15, v.tensor_tensor(T.t2[:, lo:hi], T.gg[:, lo:hi].indirect(T.iu[:, c0:c1]), T.t1[:, lo:hi], A.add))
        wm(15)
        for t in range(4):
            v.tensor_scalar(T["of%d" % t][:, lo:hi], T.t2[:, lo:hi], 4.0, T.cf[:, 2 + t:3 + t], A.mult, A.add).then_inc(S["of%d%d" % (b, t)], 1)

    seen = {"s": [], "v": []}

    def gather(key, s):
        q = sc if key == "s" else v
        role = 6 if s == own else 7 if s == par else s
        for t in range(4):
            if (t in SCALAR[role]) != (key == "s"):
                continue
            if not seen[key]:
                q.wait_ge(S.ldx, 64)
                q.wait_ge(S.vz, 1)
            sem = "of%d%d" % (s // 4, t)
            if sem not in seen[key]:
                q.wait_ge(S[sem], 1)
                seen[key].append(sem)
            out, win = T.h[:, 640 * s + t:640 * s + 640:4], T.xs[:, 0:4 * XW].indirect(T["of%d" % t][:, CD * s + 2:CD * s + 12])
            ins = sc.activation(out, win, F.Copy) if key == "s" else v.tensor_copy(out, win)
            ins.then_inc(S["hg%d" % s], 1)

    def quant(s):
        v.wait_ge(S["hg%d" % s], 4)
        cc, pp = (T.rc, T.rp) if s == own else (T.qc, T.qp)
        v.quantize_mx(cc[:, CAP * s:CAP * s + CAP], pp[:, CAP * s:CAP * s + CAP], T.h[:, 640 * s:640 * s + 640]).then_inc(S["qz%d" % s], 1)

    for s in (0, 1, 2, 3, 4, 5, par, own):
        gather("s", s)

    lists(0)
    gather("v", 0)
    quant(0)
    gather("v", 1)
    lists(1, lambda: quant(1))
    for s in (2, 4):
        gather("v", s)
        gather("v", s + 1)
        quant(s)
        quant(s + 1)
    gather("v", par)
    v.wait_ge(S.ldq, 16)
    v.quantize_mx(T.wc[:, :], T.wp[:, :], T.qs[:, :]).then_inc(S.wq, 1)
    quant(par)
    gather("v", own)

    sy.wait_ge(S.e2, 1)
    for d in range(4):
        e0 = CD * rank_at[2 * d]
        sy.dma_start(T.es[e0:e0 + 32, :], T.eb[0:1, 32 * d + 1:32 * d + 33]).then_inc(S.est, 16)
    sy.dma_start(T.el[me, CD * me:CD * me + CD, :], T.eb[0:1, CD * own + 1:CD * own + CD + 1]).then_inc(S.est, 16)

    g.wait_ge(S.est, 80)
    ids = []
    for s in [0, 1, 2, 3, 4, 5, par]:
        rid, pid, _ = topo.addr(cores[rank_at[s]])
        ids.append(DstId(rid=rid, pnc=pid))
    g.remote_dma_fused([RemoteDMATransfer(dst_ids=ids, dma_engine_mask=msk(far_e[0:1]), remote_sem=S.er, srcs=[T.es[:, :]],
                                          dsts=[T.el[me] for _ in ids])], local_sem=S.ls)
    sent[0] += 1

    def codes(s, es):
        d = there(s)
        return tr(s, es, "ar%d" % d, T.qc[:, CAP * s:CAP * s + CAP].bitcast(dt.uint8), T.rc[:, CAP * d:CAP * d + CAP].bitcast(dt.uint8))

    def plane(s, es):
        d = there(s)
        return tr(s, es, "ar%d" % d, T.qp[:, CAP * s:CAP * s + CAP], T.rp[:, CAP * d:CAP * d + CAP])

    for s in (0, 2, 4):
        g.wait_ge(S["qz%d" % s], 1)
        if s == 0:
            g.remote_dma_fused([codes(0, far_e)], local_sem=S.ls)
            g.wait_ge(S.qz1, 1)
            g.remote_dma_fused([codes(1, far_e)], local_sem=S.ls)
        else:
            g.wait_ge(S["qz%d" % (s + 1)], 1)
            g.remote_dma_fused([codes(s, far_e[0:4]), codes(s + 1, far_e[4:8])], local_sem=S.ls)
        g.remote_dma_fused([plane(s, far_e[0:4]), plane(s + 1, far_e[4:8])], local_sem=S.ls)
    g.wait_ge(S["qz%d" % par], 1)
    g.remote_dma_fused([codes(par, near_e)], local_sem=S.ls)
    g.remote_dma_fused([plane(par, near_e)], local_sem=S.ls)

    sy.wait_ge(S.est, 80)
    sy.wait_ge(S.er, 7)
    sy.wait_ge(S.rw, 1)
    for a in range(4):
        sy.dma_start(T.raw[32 * a:32 * a + 8, :], T.el[:, CD * me:CD * me + CD, :]).then_inc(S.ell, 16)
    v.wait_ge(S.ell, 64)
    op(v.tensor_copy(T.tin[:, 0:16], T.raw[:, :]))
    op(v.tensor_copy(T.tin[:, 16:32], T.raw[:, :]))
    sync_v()
    op(v.transpose(T.tout[:, :], T.tin[:, :]))
    sync_v()
    op(v.tensor_tensor(T.ef[:, 0:8], T.tout[:, 0:8], T.kk[:, 0:8], A.add))
    op(v.tensor_tensor(T.ef[:, 8:16], T.tout[:, 0:8], T.kk[:, 8:16], A.add))
    sync_v()
    op(v.tensor_copy(T.eu[:, :], T.ef[:, :]))
    sync_v()
    op(v.tensor_copy(T.msk[:, :].indirect(T.eu[:, 0:8]), T.neg[:, :]))
    quant(own)
    sync_v()

    pe.wait_ge(S.wq, 1)
    order = [0, 1, 3, 2]
    for c in order:
        for s in (2 * c, 2 * c + 1):
            if s == own:
                pe.wait_ge(S["qz%d" % own], 1)
            else:
                pe.wait_ge(S["ar%d" % s], 16 if s == par else 12 if c == 0 else 8)
        pe.matmul_mx(T.ps[:, 512 * c:512 * c + 2 * CAP], T.wc[:, :], T.wp[:, :], T.rc[:, 2 * CAP * c:2 * CAP * c + 2 * CAP],
                     T.rp[:, 2 * CAP * c:2 * CAP * c + 2 * CAP], True, True).then_inc(S["pm%d" % c], 1)
    for c in order:
        r0 = rank_at[2 * c]
        v.wait_ge(S["pm%d" % c], 1)
        op(v.tensor_tensor_scan(T.z[:, 320 * c:320 * c + 320], T.msk[:, CAP * r0:CAP * r0 + 320], T.ps[:, 512 * c:512 * c + 320],
                                NEG, A.add, A.max))
        sync_v()
        v.tensor_copy(T.ys[:, 16 * r0:16 * r0 + 32], T.z[:, 320 * c:320 * c + 320].indirect(T.eu[:, 8 + r0:10 + r0])).then_inc(S["yg%d" % c], 1)
        sy.wait_ge(S["yg%d" % c], 1)
        sy.dma_start(T.y[:, 16 * r0:16 * r0 + 32], T.ys[:, 16 * r0:16 * r0 + 32]).then_inc(S.yd, 16)
    sy.wait_ge(S.yd, 64)
    g.wait_ge(S.ls, sent[0])
